import numpy as np
import ml_dtypes

BF16 = ml_dtypes.bfloat16


def bf(x):
    return np.asarray(x, np.float32).astype(BF16)


def f32(x):
    return np.asarray(x, np.float32)


def f64(x):
    return np.asarray(x).astype(np.float64)


def striped(idx):
    return np.tile(idx.reshape(-1, 16).T, (8, 1))


S, K, M, N, E, Q, V, D = 256, 128, 512, 128, 1, 128, 128, 2


def setup_inputs():
    return {"base": bf(np.random.standard_normal((M, S))), "x": bf(np.random.standard_normal((K, N))), "w": bf(1.5 * np.random.standard_normal((E, K, M)) / np.sqrt(K)), "offs": striped(np.random.permutation(S)[:N])}


def reference(base, x, w, offs):
    idx = offs[:16].T.reshape(-1)
    z = f64(base).copy()
    for e in range(E):
        z[:, idx[e * Q : (e + 1) * Q]] += f64(w)[e].T @ f64(x)[:, e * Q : (e + 1) * Q]
    z = z
    return z.reshape(M, V, D).max(axis=2)

@@ -1,0 +1,48 @@
+import concourse.mybir as mybir
+from concourse.masks import make_identity
+
+BF16, F32, U16 = mybir.dt.bfloat16, mybir.dt.float32, mybir.dt.uint16
+MAX = mybir.AluOpType.max
+AXIS_X = mybir.AxisListType.X
+
+P = 128
+
+FLOPS = 2 * 128 * 512 * 128
+
+
+def tile_rows_unpool_max_none_kernel(tc, base, x, w, offs, out):
+    nc = tc.nc
+    features, cells = base.shape
+    points = x.shape[1]
+    pooled = out.shape[1]
+    blocks = features // P
+
+    with (
+        tc.tile_pool(name="held", bufs=1) as held,
+        tc.psum_pool(name="windows", bufs=1) as windows,
+    ):
+        base_t = held.tile([P, blocks, cells], BF16)
+        nc.sync.dma_start(base_t[:], base.rearrange("(a p) s -> p a s", p=P))
+        w_t = held.tile([P, features], BF16)
+        nc.sync.dma_start(w_t[:], w.rearrange("e k m -> (e k) m"))
+        x_t = held.tile([P, points], BF16)
+        nc.sync.dma_start(x_t[:], x)
+        offsets = held.tile([P, points // 16], U16)
+        nc.sync.dma_start(offsets[:], offs)
+
+        ident = held.tile([P, P], BF16)
+        make_identity(nc, ident[:])
+
+        z = [windows.tile([P, cells], F32, name=f"z{a}") for a in range(blocks)]
+        for a in range(blocks):
+            nc.tensor.matmul(z[a][:], ident[:], base_t[:, a, :], start=True, stop=False)
+
+        for a in range(blocks):
+            nc.tensor.matmul(
+                z[a][:].indirect(offsets[:]), w_t[:, a * P : (a + 1) * P], x_t[:], start=False, stop=True
+            )
+
+        for a in range(blocks):
+            best = held.tile([P, pooled], F32, name=f"best{a}")
+            nc.vector.tensor_reduce(best[:], z[a][:].rearrange("p (v d) -> p v d", d=cells // pooled), AXIS_X, MAX)
+            nc.sync.dma_start(out[a * P : (a + 1) * P, :], best[:])

@@ -5,6 +5,7 @@ BF16, F32, U16 = mybir.dt.bfloat16, mybir.dt.float32, mybir.dt.uint16
 MAX = mybir.AluOpType.max
 AXIS_X = mybir.AxisListType.X
 
+WARM_UPS, WARM_COLUMNS = 6, 256
 P = 128
 
 FLOPS = 2 * 128 * 512 * 128
@@ -22,13 +23,19 @@ def tile_rows_unpool_max_none_kernel(tc, base, x, w, offs, out):
         tc.psum_pool(name="windows", bufs=1) as windows,
     ):
         base_t = held.tile([P, blocks, cells], BF16)
-        nc.sync.dma_start(base_t[:], base.rearrange("(a p) s -> p a s", p=P))
+        nc.sync.dma_start(base_t[:], base.rearrange("(p a) s -> p a s", p=P))
         w_t = held.tile([P, features], BF16)
         nc.sync.dma_start(w_t[:], w.rearrange("e k m -> (e k) m"))
         x_t = held.tile([P, points], BF16)
         nc.sync.dma_start(x_t[:], x)
         offsets = held.tile([P, points // 16], U16)
         nc.sync.dma_start(offsets[:], offs)
+
+        zeros = held.tile([P, WARM_COLUMNS], BF16)
+        nc.vector.memset(zeros[:], 0.0)
+        spare = windows.tile([P, WARM_COLUMNS], F32)
+        for i in range(WARM_UPS):
+            nc.tensor.matmul(spare[:], zeros[:, :P], zeros[:], start=True, stop=True)
 
         ident = held.tile([P, P], BF16)
         make_identity(nc, ident[:])
@@ -37,12 +44,15 @@ def tile_rows_unpool_max_none_kernel(tc, base, x, w, offs, out):
         for a in range(blocks):
             nc.tensor.matmul(z[a][:], ident[:], base_t[:, a, :], start=True, stop=False)
 
+        w_by_window = w_t[:].rearrange("k (p a) -> k a p", a=blocks)
+
         for a in range(blocks):
             nc.tensor.matmul(
-                z[a][:].indirect(offsets[:]), w_t[:, a * P : (a + 1) * P], x_t[:], start=False, stop=True
+                z[a][:].indirect(offsets[:]), w_by_window[:, a, :], x_t[:], start=False, stop=True
             )
 
+        out_by_window = out.rearrange("(p a) v -> p a v", p=P)
         for a in range(blocks):
             best = held.tile([P, pooled], F32, name=f"best{a}")
             nc.vector.tensor_reduce(best[:], z[a][:].rearrange("p (v d) -> p v d", d=cells // pooled), AXIS_X, MAX)
-            nc.sync.dma_start(out[a * P : (a + 1) * P, :], best[:])
+            nc.sync.dma_start(out_by_window[:, a, :], best[:])

import concourse.mybir as mybir
from concourse.masks import make_identity

BF16, F32, U16 = mybir.dt.bfloat16, mybir.dt.float32, mybir.dt.uint16
MAX = mybir.AluOpType.max
AXIS_X = mybir.AxisListType.X

WARM_UPS, WARM_COLUMNS = 6, 256
P = 128

FLOPS = 2 * 128 * 512 * 128


def tile_rows_unpool_max_none_kernel(tc, base, x, w, offs, out):
    nc = tc.nc
    features, cells = base.shape
    points = x.shape[1]
    pooled = out.shape[1]
    blocks = features // P

    with (
        tc.tile_pool(name="held", bufs=1) as held,
        tc.psum_pool(name="windows", bufs=1) as windows,
    ):
        base_t = held.tile([P, blocks, cells], BF16)
        nc.sync.dma_start(base_t[:], base.rearrange("(p a) s -> p a s", p=P))
        w_t = held.tile([P, features], BF16)
        nc.sync.dma_start(w_t[:], w.rearrange("e k m -> (e k) m"))
        x_t = held.tile([P, points], BF16)
        nc.sync.dma_start(x_t[:], x)
        offsets = held.tile([P, points // 16], U16)
        nc.sync.dma_start(offsets[:], offs)

        zeros = held.tile([P, WARM_COLUMNS], BF16)
        nc.vector.memset(zeros[:], 0.0)
        spare = windows.tile([P, WARM_COLUMNS], F32)
        for i in range(WARM_UPS):
            nc.tensor.matmul(spare[:], zeros[:, :P], zeros[:], start=True, stop=True)

        ident = held.tile([P, P], BF16)
        make_identity(nc, ident[:])

        z = [windows.tile([P, cells], F32, name=f"z{a}") for a in range(blocks)]
        for a in range(blocks):
            nc.tensor.matmul(z[a][:], ident[:], base_t[:, a, :], start=True, stop=False)

        w_by_window = w_t[:].rearrange("k (p a) -> k a p", a=blocks)

        for a in range(blocks):
            nc.tensor.matmul(
                z[a][:].indirect(offsets[:]), w_by_window[:, a, :], x_t[:], start=False, stop=True
            )

        out_by_window = out.rearrange("(p a) v -> p a v", p=P)
        for a in range(blocks):
            best = held.tile([P, pooled], F32, name=f"best{a}")
            nc.vector.tensor_reduce(best[:], z[a][:].rearrange("p (v d) -> p v d", d=cells // pooled), AXIS_X, MAX)
            nc.sync.dma_start(out_by_window[:, a, :], best[:])
